import numpy as np
import ml_dtypes


def mxq(x, axis, fmt="e4m3"):
    dtype, down = {"e4m3": (ml_dtypes.float8_e4m3fn, 7), "e5m2": (ml_dtypes.float8_e5m2, 14)}[fmt]
    v = np.moveaxis(np.asarray(x, np.float32).astype(ml_dtypes.bfloat16).astype(np.float64), axis, -1)
    blocks = v.reshape(v.shape[:-1] + (-1, 32))
    amax = np.abs(blocks).max(-1, keepdims=True)
    byte = np.maximum(np.where(amax > 0, np.frexp(amax)[1] - 1 + 127, 0) - down, 1)
    scale = np.exp2(byte - 127.0)
    codes = (blocks / scale).astype(np.float32).astype(dtype).astype(np.float64)
    return np.moveaxis((codes * scale).reshape(v.shape), -1, axis)


WIDE = False


def mx_kscale(k):
    if not WIDE:
        return np.ones(k)
    levels = np.array([10, -10, 5, -5, 0])
    if k % 512:
        return np.exp2(np.random.permutation(np.resize(levels, k // 32))).repeat(32)
    a = np.empty((k // 512, 16))
    for p in range(k // 512):
        a[p, :8] = np.random.permutation(np.resize(levels, 8))
        for g in range(8):
            far = levels[np.abs(levels - a[p, g]) >= 10]
            a[p, g + 8] = far[np.random.randint(len(far))]
    return np.exp2(a.ravel()).repeat(32)


def f64(x):
    return np.asarray(x).astype(np.float64)


def striped(idx):
    return np.tile(idx.reshape(-1, 16).T, (8, 1)).astype(np.uint16)


def unstriped(offs):
    return offs[:16].T.reshape(-1).astype(np.int64)


E2M1 = np.array([0.0, 0.5, 1.0, 1.5, 2.0, 3.0, 4.0, 6.0, -0.0, -0.5, -1.0, -1.5, -2.0, -3.0, -4.0, -6.0])


def pack_weight(w, fmt):
    k, n = w.shape
    w = f64(np.asarray(w, np.float32).astype(ml_dtypes.bfloat16)).reshape(k // 32, 32, n)
    amax = np.abs(w).max(1)
    if fmt == "e4m3":
        byte = np.frexp(amax)[1] - 1 + 127 - 7
    else:
        mant, ex = np.frexp(amax / 6.0)
        byte = np.where(mant > 0.5, ex, ex - 1) + 127
    byte = np.clip(np.where(amax > 0, byte, 1), 1, 254)
    scaled = (w * np.exp2(127.0 - byte)[:, None, :]).reshape(k, n).astype(np.float32)
    by_word = np.ascontiguousarray(scaled.reshape(k // 512, 128, 4, n).transpose(0, 1, 3, 2))
    if fmt == "e4m3":
        words = by_word.astype(ml_dtypes.float8_e4m3fn).view(np.uint8)
    else:
        c = by_word.astype(ml_dtypes.float4_e2m1fn).view(np.uint8) & 0xF
        words = (c[..., 0::2] | (c[..., 1::2] << 4)).reshape(k // 512, 128, 2 * n)
    return np.ascontiguousarray(words), np.ascontiguousarray(byte.astype(np.uint8).reshape(k // 512, 16, n))


def unpack_weight(words, scales, fmt):
    g, _, n = scales.shape
    words = np.ascontiguousarray(words).reshape(g, 128, n, -1)
    if fmt == "e4m3":
        vals = words.view(ml_dtypes.float8_e4m3fn).astype(np.float64)
    else:
        nib = np.empty((g, 128, n, 4), np.uint8)
        nib[..., 0::2] = words & 0xF
        nib[..., 1::2] = words >> 4
        vals = E2M1[nib]
    vals = vals * np.repeat(np.exp2(scales.astype(np.float64) - 127.0), 8, axis=1)[..., None]
    return vals.transpose(0, 1, 3, 2).reshape(g * 512, n)


def gelu(v):
    return 0.5 * v * (1.0 + np.tanh(np.sqrt(2.0 / np.pi) * (v + 0.044715 * v**3)))


K, T, E, C, N = 1536, 1280, 8, 256, 128
PAD = 32


def by_expert(wq, xq):
    return np.concatenate([wq[e].T @ xq[:, e * C:(e + 1) * C] for e in range(E)], axis=1)


def setup_inputs():
    n = np.random.standard_normal
    s = mx_kscale(K)[:, None]
    first = np.random.permutation(np.repeat(np.arange(E), T // E))
    second = (first + 1 + np.random.permutation(np.repeat(np.arange(E - 1), -(-T // (E - 1)))[:T])) % E
    while np.bincount(second, minlength=E).max() != T // E:
        load = np.bincount(second, minlength=E); hi, lo = int(load.argmax()), int(load.argmin())
        t = np.flatnonzero((second == hi) & (first != lo))[0]; second[t] = lo
    slot_token = np.empty(E * C, np.int64); pos = np.empty((2, T), np.int64); fill = np.zeros(E, np.int64)
    place = np.stack([np.random.permutation(C) for _ in range(E)])
    for r, deal in enumerate((first, second)):
        for t in np.random.permutation(T):
            e = deal[t]
            if fill[e] < C: j = e * C + place[e, fill[e]]; fill[e] += 1; slot_token[j] = t; pos[r, t] = j
            else: pos[r, t] = E * C + t % PAD
    g = np.random.uniform(0.2, 0.8, T)
    w = [pack_weight(m, "e2m1") for m in n((E, K, N)) / np.sqrt(K) / s[None]]
    return {
        "xT": (n((K, T)) * s).astype(np.float32),
        "w_words": np.stack([m[0] for m in w]),
        "w_scales": np.stack([m[1] for m in w]),
        "b": (0.3 * n((N, E))).astype(np.float32),
        "gate": np.stack([np.tile(g, (N, 1)), np.tile(1.0 - g, (N, 1))]).astype(np.float32),
        "offs": striped(slot_token),
        "pos1": striped(pos[0]),
        "pos2": striped(pos[1]),
    }


def reference(xT, w_words, w_scales, b, gate, offs, pos1, pos2):
    idx = unstriped(offs)
    w = np.stack([unpack_weight(w_words[e], w_scales[e], "e2m1") for e in range(E)])
    xq = mxq(f64(xT)[:, idx], 0, "e4m3")
    y = by_expert(w, xq)
    y = gelu(y + np.repeat(f64(b), C, axis=1))
    y = np.concatenate([y, np.zeros((N, PAD))], axis=1)
    return f64(gate[0]) * y[:, unstriped(pos1)] + f64(gate[1]) * y[:, unstriped(pos2)]

@@ -1,0 +1,146 @@
+from contextlib import ExitStack
+
+import concourse.mybir as mybir
+
+K, T, E, C, N = 1536, 1280, 8, 256, 128
+S = E * C
+PAD = 32
+P = 128
+PACK = 4
+PASSES = K // (P * PACK)
+FLOPS = 2 * K * N * S
+
+F32 = mybir.dt.float32
+BF16 = mybir.dt.bfloat16
+U32 = mybir.dt.uint32
+I32 = mybir.dt.int32
+U16 = mybir.dt.uint16
+U8 = mybir.dt.uint8
+FP8X4 = mybir.dt.float8_e4m3fn_x4
+FP4X4 = mybir.dt.float4_e2m1fn_x4
+MULT = mybir.AluOpType.mult
+ADD = mybir.AluOpType.add
+COPY = mybir.ActivationFunctionType.Copy
+GELU = mybir.ActivationFunctionType.Gelu_apprx_tanh
+
+LOADS = (
+    ((0, 512), (512, 512), (1024, 256)),
+    ((0, 768), (768, 512)),
+    ((0, 512), (512, 512), (1024, 256)),
+)
+BLOCKS = (
+    ((0, 512, 256), (512, 512, 256), (1024, 256, 128)),
+    ((0, 512, 0), (512, 256, 0), (768, 512, 0)),
+    ((0, 512, 0), (512, 512, 0), (1024, 256, 0)),
+)
+PLANE_ROW = (4, 8, 0)
+SLOT_CUTS = (0, 768, 1536, 2048)
+LAST_CUTS = (0, 640, 1280, 1792, 2048)
+TOKEN_CUTS = (0, 512, 1024, 1280)
+
+
+def tile_moe_cap2_lin_gelu_kernel(tc, xT, w_words, w_scales, b, gate, offs, pos1, pos2, out):
+    nc = tc.nc
+    with ExitStack() as ctx:
+        keep = ctx.enter_context(tc.tile_pool(name="keep", bufs=1))
+        psum = ctx.enter_context(tc.psum_pool(name="psum", bufs=8))
+
+        offs_sb = keep.tile([P, S // 16], U16, name="offs_sb")
+        pos1_sb = keep.tile([P, T // 16], U16, name="pos1_sb")
+        pos2_sb = keep.tile([P, T // 16], U16, name="pos2_sb")
+        bias = keep.tile([P, E], F32, name="bias")
+        planes = keep.tile([P, T], U8, name="planes", align_bytes=64)
+        w_sb = keep.tile([P, E * PASSES, 2 * N], U8, name="w_sb", align_bytes=64)
+        ws_sb = keep.tile([P, E * PASSES, N], U8, name="ws_sb", align_bytes=64)
+        y = keep.tile([P, S + PAD], F32, name="y")
+        g0 = keep.tile([P, T], F32, name="g0")
+        g1 = keep.tile([P, T], F32, name="g1")
+        warm = keep.tile([P, 8], F32, name="warm")
+        warmed = keep.tile([P, 8], F32, name="warmed")
+
+        nc.gpsimd.memset(planes[:], 0)
+        nc.gpsimd.memset(warm[:], 0.0)
+        nc.gpsimd.memset(y[:, S:], 0.0)
+        nc.gpsimd.memset(ws_sb[:].rearrange("p g n -> p (g n)").bitcast(I32), 0)
+        nc.scalar.activation(warmed[:], warm[:], GELU)
+
+        raw = []
+        for g in range(PASSES):
+            rows = xT[g * P * PACK:(g + 1) * P * PACK, :].rearrange("(p j) t -> p j t", j=PACK)
+            raw.append(keep.tile([P, PACK, T], F32, name=f"raw{g}"))
+            for t0, width in LOADS[g]:
+                nc.sync.dma_start(raw[g][:, :, t0:t0 + width], rows[:, :, t0:t0 + width])
+            if g == 0:
+                nc.sync.dma_start(offs_sb[:], offs)
+        nc.sync.dma_start(w_sb[:].rearrange("p g n -> p g n").bitcast(I32), w_words.rearrange("e a p n -> p (e a) n").bitcast(I32))
+        for q in range(4):
+            nc.sync.dma_start(ws_sb[32 * q:32 * q + 4, :, :].bitcast(I32), w_scales[:, :, 4 * q:4 * q + 4, :].rearrange("e a q n -> q (e a) n").bitcast(I32))
+        nc.sync.dma_start(bias[:], b)
+        nc.sync.dma_start(pos1_sb[:], pos1)
+        nc.sync.dma_start(pos2_sb[:], pos2)
+        nc.sync.dma_start(g0[:], gate[0])
+        nc.sync.dma_start(g1[:], gate[1])
+
+        words = [keep.tile([P, T], U32, name=f"words{g}", align_bytes=64) for g in range(PASSES)]
+        slot_words = [keep.tile([P, S], U32, name=f"slot_words{g}", align_bytes=64) for g in range(PASSES)]
+        slot_planes = keep.tile([P, S], U8, name="slot_planes", align_bytes=64)
+        moved = [keep.tile([P, S], U8, name=f"moved{g}", align_bytes=64) for g in range(PASSES - 1)]
+
+        def gather_words(g, a, z):
+            nc.vector.tensor_copy(slot_words[g][:, a:z], words[g][:].indirect(offs_sb[:, a // 16:z // 16]))
+
+        for g in range(PASSES):
+            k = PLANE_ROW[g]
+            for c, (t0, width, v) in enumerate(BLOCKS[g]):
+                mixed = keep.tile([P, width, PACK], BF16, name=f"mixed{g}_{c}", align_bytes=64)
+                src = raw[g][:, :, t0:t0 + width].rearrange("p j t -> p t j")
+                nc.scalar.activation(mixed[:, v:, :], src[:, v:, :], COPY)
+                if v > 0:
+                    nc.vector.tensor_copy(mixed[:, :v, :], src[:, :v, :])
+                nc.vector.quantize_mx(
+                    out=words[g][:, t0:t0 + width].bitcast(FP8X4),
+                    scales=planes[k:P, t0:t0 + width],
+                    in_=mixed[:].rearrange("p t j -> p (t j)"),
+                )
+            if g < PASSES - 1:
+                for a, z in zip(SLOT_CUTS, SLOT_CUTS[1:]):
+                    gather_words(g, a, z)
+
+        for a, z in zip(SLOT_CUTS, SLOT_CUTS[1:]):
+            nc.vector.tensor_copy(slot_planes[:, a:z], planes[:].indirect(offs_sb[:, a // 16:z // 16]))
+            for g in range(PASSES - 1):
+                k = PLANE_ROW[g]
+                nc.sync.dma_start(moved[g][0:P - k, a:z].bitcast(I32), slot_planes[k:P, a:z].bitcast(I32))
+
+        for a, z in zip(LAST_CUTS, LAST_CUTS[1:]):
+            gather_words(PASSES - 1, a, z)
+
+        scale_planes = (moved[0], moved[1], slot_planes)
+        for e in range(E):
+            last = e == E - 1
+            acc = psum.tile([P, C], F32, name="acc")
+            accs = (acc, psum.tile([P, C], F32, name="acc") if last else acc)
+            order = [(h, g) for g in range(PASSES) for h in range(2)] if last else [(h, g) for h in range(2) for g in range(PASSES)]
+            for h, g in order:
+                s0 = e * C + h * P
+                if True:
+                    nc.tensor.matmul_mx(
+                        out=accs[h][:, h * P:(h + 1) * P],
+                        lhsT=w_sb[:, e * PASSES + g, :].bitcast(FP4X4),
+                        lhsT_scale=ws_sb[:, e * PASSES + g, :],
+                        rhs=slot_words[g][:, s0:s0 + P].bitcast(FP8X4),
+                        rhs_scale=scale_planes[g][:, s0:s0 + P],
+                        start=(g == 0),
+                        stop=(g == PASSES - 1),
+                    )
+            for a, z in ((0, P), (P, C)) if last else ((0, C),):
+                nc.scalar.activation(y[:, e * C + a:e * C + z], accs[a // P][:, a:z], GELU, bias=bias[:, e:e + 1])
+
+        for a, z in zip(TOKEN_CUTS, TOKEN_CUTS[1:]):
+            r0 = keep.tile([P, z - a], F32, name=f"r0_{a}")
+            r1 = keep.tile([P, z - a], F32, name=f"r1_{a}")
+            res = keep.tile([P, z - a], F32, name=f"res_{a}")
+            nc.vector.tensor_tensor(r0[:], y[:].indirect(pos1_sb[:, a // 16:z // 16]), g0[:, a:z], MULT)
+            nc.vector.tensor_tensor(r1[:], y[:].indirect(pos2_sb[:, a // 16:z // 16]), g1[:, a:z], MULT)
+            nc.vector.tensor_tensor(res[:], r0[:], r1[:], ADD)
+            nc.sync.dma_start(out[:, a:z], res[:])

@@ -23,15 +23,10 @@ ADD = mybir.AluOpType.add
 COPY = mybir.ActivationFunctionType.Copy
 GELU = mybir.ActivationFunctionType.Gelu_apprx_tanh
 
-LOADS = (
-    ((0, 512), (512, 512), (1024, 256)),
-    ((0, 768), (768, 512)),
-    ((0, 512), (512, 512), (1024, 256)),
-)
 BLOCKS = (
     ((0, 512, 256), (512, 512, 256), (1024, 256, 128)),
-    ((0, 512, 0), (512, 256, 0), (768, 512, 0)),
-    ((0, 512, 0), (512, 512, 0), (1024, 256, 0)),
+    ((0, 256, 0), (256, 512, 0), (768, 512, 0)),
+    ((0, 512, 0), (512, 512, 0), (1024, 256, 128)),
 )
 PLANE_ROW = (4, 8, 0)
 SLOT_CUTS = (0, 768, 1536, 2048)
@@ -67,9 +62,11 @@ def tile_moe_cap2_lin_gelu_kernel(tc, xT, w_words, w_scales, b, gate, offs, pos1
         raw = []
         for g in range(PASSES):
             rows = xT[g * P * PACK:(g + 1) * P * PACK, :].rearrange("(p j) t -> p j t", j=PACK)
-            raw.append(keep.tile([P, PACK, T], F32, name=f"raw{g}"))
-            for t0, width in LOADS[g]:
-                nc.sync.dma_start(raw[g][:, :, t0:t0 + width], rows[:, :, t0:t0 + width])
+            raw.append([])
+            for c, (t0, width, v) in enumerate(BLOCKS[g]):
+                piece = keep.tile([P, PACK, width], F32, name=f"raw{g}_{c}")
+                nc.sync.dma_start(piece[:], rows[:, :, t0:t0 + width])
+                raw[g].append(piece)
             if g == 0:
                 nc.sync.dma_start(offs_sb[:], offs)
         nc.sync.dma_start(w_sb[:].rearrange("p g n -> p g n").bitcast(I32), w_words.rearrange("e a p n -> p (e a) n").bitcast(I32))
@@ -93,10 +90,14 @@ def tile_moe_cap2_lin_gelu_kernel(tc, xT, w_words, w_scales, b, gate, offs, pos1
             k = PLANE_ROW[g]
             for c, (t0, width, v) in enumerate(BLOCKS[g]):
                 mixed = keep.tile([P, width, PACK], BF16, name=f"mixed{g}_{c}", align_bytes=64)
-                src = raw[g][:, :, t0:t0 + width].rearrange("p j t -> p t j")
-                nc.scalar.activation(mixed[:, v:, :], src[:, v:, :], COPY)
+                src = raw[g][c][:]
+                nc.scalar.activation(
+                    mixed[:, v:, :].rearrange("p (c i) j -> p c j i", i=4), src[:, :, v:].rearrange("p j (c i) -> p c j i", i=4), COPY
+                )
                 if v > 0:
-                    nc.vector.tensor_copy(mixed[:, :v, :], src[:, :v, :])
+                    nc.vector.tensor_copy(
+                        mixed[:, :v, :].rearrange("p (c i) j -> p c j i", i=4), src[:, :, :v].rearrange("p j (c i) -> p c j i", i=4)
+                    )
                 nc.vector.quantize_mx(
                     out=words[g][:, t0:t0 + width].bitcast(FP8X4),
                     scales=planes[k:P, t0:t0 + width],
@@ -106,11 +107,12 @@ def tile_moe_cap2_lin_gelu_kernel(tc, xT, w_words, w_scales, b, gate, offs, pos1
                 for a, z in zip(SLOT_CUTS, SLOT_CUTS[1:]):
                     gather_words(g, a, z)
 
-        for a, z in zip(SLOT_CUTS, SLOT_CUTS[1:]):
+        for a, z, moves in ((0, 640, None), (640, 1280, (0, 1280)), (1280, 2048, (1280, 2048))):
             nc.vector.tensor_copy(slot_planes[:, a:z], planes[:].indirect(offs_sb[:, a // 16:z // 16]))
-            for g in range(PASSES - 1):
-                k = PLANE_ROW[g]
-                nc.sync.dma_start(moved[g][0:P - k, a:z].bitcast(I32), slot_planes[k:P, a:z].bitcast(I32))
+            if moves:
+                m, n = moves
+                nc.sync.dma_start(moved[0][0:124, m:n].bitcast(I32), slot_planes[4:P, m:n].bitcast(I32))
+                nc.sync.dma_start(moved[1][0:120, m:n].bitcast(I32), slot_planes[8:P, m:n].bitcast(I32))
 
         for a, z in zip(LAST_CUTS, LAST_CUTS[1:]):
             gather_words(PASSES - 1, a, z)

@@ -28,10 +28,10 @@ BLOCKS = (
     ((0, 256, 0), (256, 512, 0), (768, 512, 0)),
     ((0, 512, 0), (512, 512, 0), (1024, 256, 128)),
 )
-PLANE_ROW = (4, 8, 0)
+PLANE_ROW = (0, 4, 8)
 SLOT_CUTS = (0, 768, 1536, 2048)
 LAST_CUTS = (0, 640, 1280, 1792, 2048)
-TOKEN_CUTS = (0, 512, 1024, 1280)
+TOKEN_CUTS = (0, 640, 1024, 1280)
 
 
 def tile_moe_cap2_lin_gelu_kernel(tc, xT, w_words, w_scales, b, gate, offs, pos1, pos2, out):
@@ -81,7 +81,7 @@ def tile_moe_cap2_lin_gelu_kernel(tc, xT, w_words, w_scales, b, gate, offs, pos1
         words = [keep.tile([P, T], U32, name=f"words{g}", align_bytes=64) for g in range(PASSES)]
         slot_words = [keep.tile([P, S], U32, name=f"slot_words{g}", align_bytes=64) for g in range(PASSES)]
         slot_planes = keep.tile([P, S], U8, name="slot_planes", align_bytes=64)
-        moved = [keep.tile([P, S], U8, name=f"moved{g}", align_bytes=64) for g in range(PASSES - 1)]
+        moved = [slot_planes] + [keep.tile([P, S], U8, name=f"moved{g}", align_bytes=64) for g in range(1, PASSES)]
 
         def gather_words(g, a, z):
             nc.vector.tensor_copy(slot_words[g][:, a:z], words[g][:].indirect(offs_sb[:, a // 16:z // 16]))
@@ -111,38 +111,72 @@ def tile_moe_cap2_lin_gelu_kernel(tc, xT, w_words, w_scales, b, gate, offs, pos1
             nc.vector.tensor_copy(slot_planes[:, a:z], planes[:].indirect(offs_sb[:, a // 16:z // 16]))
             if moves:
                 m, n = moves
-                nc.sync.dma_start(moved[0][0:124, m:n].bitcast(I32), slot_planes[4:P, m:n].bitcast(I32))
-                nc.sync.dma_start(moved[1][0:120, m:n].bitcast(I32), slot_planes[8:P, m:n].bitcast(I32))
+                for g in (1, 2):
+                    k = PLANE_ROW[g]
+                    for r, rows in ((0, 64), (64, 32), (96, 16)):
+                        nc.sync.dma_start(moved[g][r:r + rows, m:n].bitcast(I32), slot_planes[r + k:r + k + rows, m:n].bitcast(I32))
 
         for a, z in zip(LAST_CUTS, LAST_CUTS[1:]):
             gather_words(PASSES - 1, a, z)
 
-        scale_planes = (moved[0], moved[1], slot_planes)
-        for e in range(E):
-            last = e == E - 1
-            acc = psum.tile([P, C], F32, name="acc")
-            accs = (acc, psum.tile([P, C], F32, name="acc") if last else acc)
-            order = [(h, g) for g in range(PASSES) for h in range(2)] if last else [(h, g) for h in range(2) for g in range(PASSES)]
-            for h, g in order:
-                s0 = e * C + h * P
-                if True:
-                    nc.tensor.matmul_mx(
-                        out=accs[h][:, h * P:(h + 1) * P],
-                        lhsT=w_sb[:, e * PASSES + g, :].bitcast(FP4X4),
-                        lhsT_scale=ws_sb[:, e * PASSES + g, :],
-                        rhs=slot_words[g][:, s0:s0 + P].bitcast(FP8X4),
-                        rhs_scale=scale_planes[g][:, s0:s0 + P],
-                        start=(g == 0),
-                        stop=(g == PASSES - 1),
-                    )
-            for a, z in ((0, P), (P, C)) if last else ((0, C),):
-                nc.scalar.activation(y[:, e * C + a:e * C + z], accs[a // P][:, a:z], GELU, bias=bias[:, e:e + 1])
+        def multiply(acc, e, h, g):
+            s0 = e * C + h * P
+            nc.tensor.matmul_mx(
+                out=acc[:, h * P:(h + 1) * P],
+                lhsT=w_sb[:, e * PASSES + g, :].bitcast(FP4X4),
+                lhsT_scale=ws_sb[:, e * PASSES + g, :],
+                rhs=slot_words[g][:, s0:s0 + P].bitcast(FP8X4),
+                rhs_scale=moved[g][:, s0:s0 + P],
+                start=(g == 0),
+                stop=(g == PASSES - 1),
+            )
 
-        for a, z in zip(TOKEN_CUTS, TOKEN_CUTS[1:]):
-            r0 = keep.tile([P, z - a], F32, name=f"r0_{a}")
-            r1 = keep.tile([P, z - a], F32, name=f"r1_{a}")
-            res = keep.tile([P, z - a], F32, name=f"res_{a}")
-            nc.vector.tensor_tensor(r0[:], y[:].indirect(pos1_sb[:, a // 16:z // 16]), g0[:, a:z], MULT)
-            nc.vector.tensor_tensor(r1[:], y[:].indirect(pos2_sb[:, a // 16:z // 16]), g1[:, a:z], MULT)
-            nc.vector.tensor_tensor(res[:], r0[:], r1[:], ADD)
+        def finish(acc, e, a, z):
+            nc.scalar.activation(y[:, e * C + a:e * C + z], acc[:, a:z], GELU, bias=bias[:, e:e + 1])
+
+        accs = [psum.tile([P, C], F32, name="acc") for e in range(E)]
+        for e in range(E):
+            multiply(accs[e], e, 0, 0)
+        for e in range(5):
+            multiply(accs[e], e, 0, 1)
+        for e in range(E - 1):
+            if e >= 5:
+                multiply(accs[e], e, 0, 1)
+            multiply(accs[e], e, 0, 2)
+            for g in range(PASSES):
+                multiply(accs[e], e, 1, g)
+            finish(accs[e], e, 0, C)
+        e = E - 1
+        extra = psum.tile([P, C], F32, name="acc")
+        multiply(accs[e], e, 0, 1)
+        multiply(extra, e, 1, 0)
+        multiply(extra, e, 1, 1)
+        multiply(accs[e], e, 0, 2)
+        finish(accs[e], e, 0, P)
+        multiply(extra, e, 1, 2)
+        finish(extra, e, P, C)
+
+        parts = list(zip(TOKEN_CUTS, TOKEN_CUTS[1:]))
+        lists = (pos1_sb, pos2_sb)
+        gates = (g0, g1)
+        picked = [[keep.tile([P, z - a], F32, name=f"picked{r}_{a}") for r in range(2)] for a, z in parts]
+
+        def pick(i, r):
+            a, z = parts[i]
+            nc.vector.tensor_tensor(picked[i][r][:], y[:].indirect(lists[r][:, a // 16:z // 16]), gates[r][:, a:z], MULT)
+
+        def combine(i):
+            a, z = parts[i]
+            res = keep.tile([P, z - a], F32, name=f"res{i}")
+            nc.vector.tensor_tensor(res[:], picked[i][0][:], picked[i][1][:], ADD)
             nc.sync.dma_start(out[:, a:z], res[:])
+
+        pick(0, 0)
+        pick(0, 1)
+        pick(1, 0)
+        combine(0)
+        pick(1, 1)
+        pick(2, 0)
+        pick(2, 1)
+        combine(1)
+        combine(2)

from contextlib import ExitStack

import concourse.mybir as mybir

K, T, E, C, N = 1536, 1280, 8, 256, 128
S = E * C
PAD = 32
P = 128
PACK = 4
PASSES = K // (P * PACK)
FLOPS = 2 * K * N * S

F32 = mybir.dt.float32
BF16 = mybir.dt.bfloat16
U32 = mybir.dt.uint32
I32 = mybir.dt.int32
U16 = mybir.dt.uint16
U8 = mybir.dt.uint8
FP8X4 = mybir.dt.float8_e4m3fn_x4
FP4X4 = mybir.dt.float4_e2m1fn_x4
MULT = mybir.AluOpType.mult
ADD = mybir.AluOpType.add
COPY = mybir.ActivationFunctionType.Copy
GELU = mybir.ActivationFunctionType.Gelu_apprx_tanh

BLOCKS = (
    ((0, 512, 256), (512, 512, 256), (1024, 256, 128)),
    ((0, 256, 0), (256, 512, 0), (768, 512, 0)),
    ((0, 512, 0), (512, 512, 0), (1024, 256, 128)),
)
PLANE_ROW = (0, 4, 8)
SLOT_CUTS = (0, 768, 1536, 2048)
LAST_CUTS = (0, 640, 1280, 1792, 2048)
TOKEN_CUTS = (0, 640, 1024, 1280)


def tile_moe_cap2_lin_gelu_kernel(tc, xT, w_words, w_scales, b, gate, offs, pos1, pos2, out):
    nc = tc.nc
    with ExitStack() as ctx:
        keep = ctx.enter_context(tc.tile_pool(name="keep", bufs=1))
        psum = ctx.enter_context(tc.psum_pool(name="psum", bufs=8))

        offs_sb = keep.tile([P, S // 16], U16, name="offs_sb")
        pos1_sb = keep.tile([P, T // 16], U16, name="pos1_sb")
        pos2_sb = keep.tile([P, T // 16], U16, name="pos2_sb")
        bias = keep.tile([P, E], F32, name="bias")
        planes = keep.tile([P, T], U8, name="planes", align_bytes=64)
        w_sb = keep.tile([P, E * PASSES, 2 * N], U8, name="w_sb", align_bytes=64)
        ws_sb = keep.tile([P, E * PASSES, N], U8, name="ws_sb", align_bytes=64)
        y = keep.tile([P, S + PAD], F32, name="y")
        g0 = keep.tile([P, T], F32, name="g0")
        g1 = keep.tile([P, T], F32, name="g1")
        warm = keep.tile([P, 8], F32, name="warm")
        warmed = keep.tile([P, 8], F32, name="warmed")

        nc.gpsimd.memset(planes[:], 0)
        nc.gpsimd.memset(warm[:], 0.0)
        nc.gpsimd.memset(y[:, S:], 0.0)
        nc.gpsimd.memset(ws_sb[:].rearrange("p g n -> p (g n)").bitcast(I32), 0)
        nc.scalar.activation(warmed[:], warm[:], GELU)

        raw = []
        for g in range(PASSES):
            rows = xT[g * P * PACK:(g + 1) * P * PACK, :].rearrange("(p j) t -> p j t", j=PACK)
            raw.append([])
            for c, (t0, width, v) in enumerate(BLOCKS[g]):
                piece = keep.tile([P, PACK, width], F32, name=f"raw{g}_{c}")
                nc.sync.dma_start(piece[:], rows[:, :, t0:t0 + width])
                raw[g].append(piece)
            if g == 0:
                nc.sync.dma_start(offs_sb[:], offs)
        nc.sync.dma_start(w_sb[:].rearrange("p g n -> p g n").bitcast(I32), w_words.rearrange("e a p n -> p (e a) n").bitcast(I32))
        for q in range(4):
            nc.sync.dma_start(ws_sb[32 * q:32 * q + 4, :, :].bitcast(I32), w_scales[:, :, 4 * q:4 * q + 4, :].rearrange("e a q n -> q (e a) n").bitcast(I32))
        nc.sync.dma_start(bias[:], b)
        nc.sync.dma_start(pos1_sb[:], pos1)
        nc.sync.dma_start(pos2_sb[:], pos2)
        nc.sync.dma_start(g0[:], gate[0])
        nc.sync.dma_start(g1[:], gate[1])

        words = [keep.tile([P, T], U32, name=f"words{g}", align_bytes=64) for g in range(PASSES)]
        slot_words = [keep.tile([P, S], U32, name=f"slot_words{g}", align_bytes=64) for g in range(PASSES)]
        slot_planes = keep.tile([P, S], U8, name="slot_planes", align_bytes=64)
        moved = [slot_planes] + [keep.tile([P, S], U8, name=f"moved{g}", align_bytes=64) for g in range(1, PASSES)]

        def gather_words(g, a, z):
            nc.vector.tensor_copy(slot_words[g][:, a:z], words[g][:].indirect(offs_sb[:, a // 16:z // 16]))

        for g in range(PASSES):
            k = PLANE_ROW[g]
            for c, (t0, width, v) in enumerate(BLOCKS[g]):
                mixed = keep.tile([P, width, PACK], BF16, name=f"mixed{g}_{c}", align_bytes=64)
                src = raw[g][c][:]
                nc.scalar.activation(
                    mixed[:, v:, :].rearrange("p (c i) j -> p c j i", i=4), src[:, :, v:].rearrange("p j (c i) -> p c j i", i=4), COPY
                )
                if v > 0:
                    nc.vector.tensor_copy(
                        mixed[:, :v, :].rearrange("p (c i) j -> p c j i", i=4), src[:, :, :v].rearrange("p j (c i) -> p c j i", i=4)
                    )
                nc.vector.quantize_mx(
                    out=words[g][:, t0:t0 + width].bitcast(FP8X4),
                    scales=planes[k:P, t0:t0 + width],
                    in_=mixed[:].rearrange("p t j -> p (t j)"),
                )
            if g < PASSES - 1:
                for a, z in zip(SLOT_CUTS, SLOT_CUTS[1:]):
                    gather_words(g, a, z)

        for a, z, moves in ((0, 640, None), (640, 1280, (0, 1280)), (1280, 2048, (1280, 2048))):
            nc.vector.tensor_copy(slot_planes[:, a:z], planes[:].indirect(offs_sb[:, a // 16:z // 16]))
            if moves:
                m, n = moves
                for g in (1, 2):
                    k = PLANE_ROW[g]
                    for r, rows in ((0, 64), (64, 32), (96, 16)):
                        nc.sync.dma_start(moved[g][r:r + rows, m:n].bitcast(I32), slot_planes[r + k:r + k + rows, m:n].bitcast(I32))

        for a, z in zip(LAST_CUTS, LAST_CUTS[1:]):
            gather_words(PASSES - 1, a, z)

        def multiply(acc, e, h, g):
            s0 = e * C + h * P
            nc.tensor.matmul_mx(
                out=acc[:, h * P:(h + 1) * P],
                lhsT=w_sb[:, e * PASSES + g, :].bitcast(FP4X4),
                lhsT_scale=ws_sb[:, e * PASSES + g, :],
                rhs=slot_words[g][:, s0:s0 + P].bitcast(FP8X4),
                rhs_scale=moved[g][:, s0:s0 + P],
                start=(g == 0),
                stop=(g == PASSES - 1),
            )

        def finish(acc, e, a, z):
            nc.scalar.activation(y[:, e * C + a:e * C + z], acc[:, a:z], GELU, bias=bias[:, e:e + 1])

        accs = [psum.tile([P, C], F32, name="acc") for e in range(E)]
        for e in range(E):
            multiply(accs[e], e, 0, 0)
        for e in range(5):
            multiply(accs[e], e, 0, 1)
        for e in range(E - 1):
            if e >= 5:
                multiply(accs[e], e, 0, 1)
            multiply(accs[e], e, 0, 2)
            for g in range(PASSES):
                multiply(accs[e], e, 1, g)
            finish(accs[e], e, 0, C)
        e = E - 1
        extra = psum.tile([P, C], F32, name="acc")
        multiply(accs[e], e, 0, 1)
        multiply(extra, e, 1, 0)
        multiply(extra, e, 1, 1)
        multiply(accs[e], e, 0, 2)
        finish(accs[e], e, 0, P)
        multiply(extra, e, 1, 2)
        finish(extra, e, P, C)

        parts = list(zip(TOKEN_CUTS, TOKEN_CUTS[1:]))
        lists = (pos1_sb, pos2_sb)
        gates = (g0, g1)
        picked = [[keep.tile([P, z - a], F32, name=f"picked{r}_{a}") for r in range(2)] for a, z in parts]

        def pick(i, r):
            a, z = parts[i]
            nc.vector.tensor_tensor(picked[i][r][:], y[:].indirect(lists[r][:, a // 16:z // 16]), gates[r][:, a:z], MULT)

        def combine(i):
            a, z = parts[i]
            res = keep.tile([P, z - a], F32, name=f"res{i}")
            nc.vector.tensor_tensor(res[:], picked[i][0][:], picked[i][1][:], ADD)
            nc.sync.dma_start(out[:, a:z], res[:])

        pick(0, 0)
        pick(0, 1)
        pick(1, 0)
        combine(0)
        pick(1, 1)
        pick(2, 0)
        pick(2, 1)
        combine(1)
        combine(2)
